import numpy as np
import ml_dtypes


def mxq(x, axis, fmt="e4m3"):
    dtype, down = {"e4m3": (ml_dtypes.float8_e4m3fn, 7), "e5m2": (ml_dtypes.float8_e5m2, 14)}[fmt]
    v = np.moveaxis(np.asarray(x, np.float32).astype(ml_dtypes.bfloat16).astype(np.float64), axis, -1)
    blocks = v.reshape(v.shape[:-1] + (-1, 32))
    amax = np.abs(blocks).max(-1, keepdims=True)
    byte = np.maximum(np.where(amax > 0, np.frexp(amax)[1] - 1 + 127, 0) - down, 1)
    scale = np.exp2(byte - 127.0)
    codes = (blocks / scale).astype(np.float32).astype(dtype).astype(np.float64)
    return np.moveaxis((codes * scale).reshape(v.shape), -1, axis)


WIDE = False


def mx_kscale(k):
    if not WIDE:
        return np.ones(k)
    levels = np.array([10, -10, 5, -5, 0])
    if k % 512:
        return np.exp2(np.random.permutation(np.resize(levels, k // 32))).repeat(32)
    a = np.empty((k // 512, 16))
    for p in range(k // 512):
        a[p, :8] = np.random.permutation(np.resize(levels, 8))
        for g in range(8):
            far = levels[np.abs(levels - a[p, g]) >= 10]
            a[p, g + 8] = far[np.random.randint(len(far))]
    return np.exp2(a.ravel()).repeat(32)


def f64(x):
    return np.asarray(x).astype(np.float64)


def striped(idx):
    return np.tile(np.asarray(idx).reshape(-1, 16).T, (8, 1)).astype(np.uint16)


def unstriped(offs):
    return offs[:16].T.reshape(-1).astype(np.int64)


E2M1 = np.array([0.0, 0.5, 1.0, 1.5, 2.0, 3.0, 4.0, 6.0, -0.0, -0.5, -1.0, -1.5, -2.0, -3.0, -4.0, -6.0])


def pack_weight(w, fmt):
    k, n = w.shape
    w = f64(np.asarray(w, np.float32).astype(ml_dtypes.bfloat16)).reshape(k // 32, 32, n)
    amax = np.abs(w).max(1)
    if fmt == "e4m3":
        byte = np.frexp(amax)[1] - 1 + 127 - 7
    else:
        mant, ex = np.frexp(amax / 6.0)
        byte = np.where(mant > 0.5, ex, ex - 1) + 127
    byte = np.clip(np.where(amax > 0, byte, 1), 1, 254)
    scaled = (w * np.exp2(127.0 - byte)[:, None, :]).reshape(k, n).astype(np.float32)
    by_word = np.ascontiguousarray(scaled.reshape(k // 512, 128, 4, n).transpose(0, 1, 3, 2))
    if fmt == "e4m3":
        words = by_word.astype(ml_dtypes.float8_e4m3fn).view(np.uint8)
    else:
        c = by_word.astype(ml_dtypes.float4_e2m1fn).view(np.uint8) & 0xF
        words = (c[..., 0::2] | (c[..., 1::2] << 4)).reshape(k // 512, 128, 2 * n)
    return np.ascontiguousarray(words), np.ascontiguousarray(byte.astype(np.uint8).reshape(k // 512, 16, n))


def unpack_weight(words, scales, fmt):
    g, _, n = scales.shape
    words = np.ascontiguousarray(words).reshape(g, 128, n, -1)
    if fmt == "e4m3":
        vals = words.view(ml_dtypes.float8_e4m3fn).astype(np.float64)
    else:
        nib = np.empty((g, 128, n, 4), np.uint8)
        nib[..., 0::2] = words & 0xF
        nib[..., 1::2] = words >> 4
        vals = E2M1[nib]
    vals = vals * np.repeat(np.exp2(scales.astype(np.float64) - 127.0), 8, axis=1)[..., None]
    return vals.transpose(0, 1, 3, 2).reshape(g * 512, n)


D, E, T, I, Q = 512, 512, 1024, 256, 512


def setup_inputs():
    n = np.random.standard_normal
    idx = np.random.permutation(T)[:I]
    fd = mx_kscale(D)
    fq = mx_kscale(Q)
    keysp = pack_weight(n((D, T)) / fd[:, None], "e2m1")
    return {
        "query": (n((D, Q)) * 1.0 / np.sqrt(D) * fd[:, None]).astype(np.float32),
        "keys_words": keysp[0],
        "keys_scales": keysp[1],
        "floor": (np.random.uniform(0.05, 0.3, (Q, 1))).astype(np.float32),
        "reserve": (np.random.uniform(20.0, 100.0, (Q, 1))).astype(np.float32),
        "qs": (np.random.uniform(2.0, 8.0, (Q, 1)) * fq[:, None]).astype(np.float32),
        "grows": (n((Q, E)) / fq[:, None]).astype(np.float32),
        "old": (n((E, T)) * 2.0).astype(np.float32),
        "fade": (np.random.uniform(0.5, 1.0, (1, T))).astype(np.float32),
        "offs": striped(idx),
    }


def reference(query, keys_words, keys_scales, floor, reserve, qs, grows, old, fade, offs):
    idx = unstriped(offs)
    keysu = unpack_weight(keys_words, keys_scales, "e2m1")
    queryq = mxq(f64(query), 0, "e4m3")
    keysidxg = keysu[:, idx]
    a = queryq.T @ keysidxg
    p = np.square(a) + f64(floor)
    z = np.sum(p, axis=1, keepdims=True) + f64(reserve)
    w = p / z
    wq = w * f64(qs)
    growsq = mxq(f64(grows), 0, "e4m3")
    wqq = mxq(wq, 0, "e4m3")
    gv = growsq.T @ wqq
    gf = np.zeros((E, T))
    gf[:, idx] = gv
    y = f64(old) * f64(fade) + gf
    return y

@@ -1,0 +1,168 @@
+from contextlib import ExitStack
+
+import concourse.mybir as mybir
+from concourse.masks import make_identity
+
+D, E, T, I, Q = 512, 512, 1024, 256, 512
+FLOPS = 2 * D * Q * I + 2 * Q * E * I
+
+F32 = mybir.dt.float32
+BF16 = mybir.dt.bfloat16
+I32 = mybir.dt.int32
+U32 = mybir.dt.uint32
+U16 = mybir.dt.uint16
+U8 = mybir.dt.uint8
+FP8X4 = mybir.dt.float8_e4m3fn_x4
+FP4X4 = mybir.dt.float4_e2m1fn_x4
+ALU = mybir.AluOpType
+ACT = mybir.ActivationFunctionType
+
+P = 128
+PACK = 4
+BANK = 512
+
+
+def tile_attend_bsquareshares_v_kernel(tc, query, keys_words, keys_scales, floor, reserve, qs, grows, old, fade, offs, out):
+    nc = tc.nc
+    with ExitStack() as ctx:
+        sb = ctx.enter_context(tc.tile_pool(name="sb", bufs=1))
+        ps = ctx.enter_context(tc.psum_pool(name="ps", bufs=1))
+
+        offsets = sb.tile([P, I // 16], U16, name="offsets")
+        nc.sync.dma_start(offsets[:], offs)
+        key_words = sb.tile([P, T], U16, name="key_words", align_bytes=64)
+        nc.sync.dma_start(key_words[:].bitcast(I32), keys_words[0].bitcast(I32))
+        key_bytes = sb.tile([P, T], U8, name="key_bytes", align_bytes=64)
+        nc.vector.memset(key_bytes[:].bitcast(I32), 0)
+        for quad in range(4):
+            nc.scalar.dma_start(
+                key_bytes[32 * quad : 32 * quad + 4, :].bitcast(I32),
+                keys_scales[0, 4 * quad : 4 * quad + 4, :].bitcast(I32),
+            )
+        q_rows = query.rearrange("(p j) q -> p j q", j=PACK)
+        q_raw = []
+        for h in range(2):
+            t = sb.tile([P, PACK, Q // 2], F32, name=f"q_raw{h}")
+            nc.sync.dma_start(t[:], q_rows[:, :, h * (Q // 2) : (h + 1) * (Q // 2)])
+            q_raw.append(t)
+        floor_sb = sb.tile([P, PACK], F32, name="floor_sb")
+        reserve_sb = sb.tile([P, PACK], F32, name="reserve_sb")
+        qs_sb = sb.tile([P, PACK], F32, name="qs_sb")
+        for t, src in ((floor_sb, floor), (reserve_sb, reserve), (qs_sb, qs)):
+            nc.sync.dma_start(t[:], src.rearrange("(p r) o -> p (r o)", r=PACK))
+        fade_cols = sb.tile([P, 2, PACK], F32, name="fade_cols")
+        nc.sync.dma_start(fade_cols[:], fade.rearrange("o (h p j) -> p (o h) j", h=2, j=PACK))
+        g_raw = sb.tile([P, PACK, E], F32, name="g_raw")
+        nc.sync.dma_start(g_raw[:], grows.rearrange("(p j) e -> p j e", j=PACK))
+        acc = []
+        for c in range(E // P):
+            t = sb.tile([P, T], F32, name=f"acc{c}")
+            nc.sync.dma_start(t[:], old[c * P : (c + 1) * P, :])
+            acc.append(t)
+
+        windows = []
+        for c in range(E // P):
+            t = sb.tile([P, T], F32, name=f"window{c}")
+            nc.vector.memset(t[:], 0.0)
+            windows.append(t)
+        ident = sb.tile([P, P], F32, name="ident")
+        make_identity(nc, ident[:])
+
+        k_words = sb.tile([P, I], U16, name="k_words", align_bytes=64)
+        k_bytes = sb.tile([P, I], U8, name="k_bytes", align_bytes=64)
+        nc.vector.tensor_copy(k_words[:], key_words[:].indirect(offsets[:]))
+        nc.vector.tensor_copy(k_bytes[:], key_bytes[:].indirect(offsets[:]))
+
+        q_bf = sb.tile([P, PACK, P, PACK], BF16, name="q_bf", align_bytes=64)
+        for h in range(2):
+            dst = q_bf[:, :, h * 64 : (h + 1) * 64, :].rearrange("p r s j -> p s j r")
+            src = q_raw[h][:].rearrange("p j (s r) -> p s j r", r=PACK)
+            if h == 0:
+                nc.scalar.copy(dst, src)
+            else:
+                nc.vector.tensor_copy(dst, src)
+        base = sb.tile([P, PACK], F32, name="base")
+        nc.vector.scalar_tensor_tensor(base[:], floor_sb[:], float(I), reserve_sb[:], ALU.mult, ALU.add)
+
+        sq = sb.tile([P, PACK, I], F32, name="sq")
+        x = sb.tile([P, PACK, I], F32, name="x")
+        sums = sb.tile([P, PACK], F32, name="sums")
+        for r in range(PACK):
+            q_codes = sb.tile([P, P], U32, name=f"q_codes{r}", align_bytes=64)
+            q_scales = sb.tile([P, P], U8, name=f"q_scales{r}", align_bytes=64)
+            nc.vector.quantize_mx(
+                out=q_codes[:].bitcast(FP8X4), scales=q_scales[:], in_=q_bf[:, r].rearrange("p s j -> p (s j)")
+            )
+            score = ps.tile([P, I], F32, name=f"score{r}", tag=f"bank{r}")
+            nc.tensor.matmul_mx(
+                out=score[:],
+                lhsT=q_codes[:].bitcast(FP8X4),
+                lhsT_scale=q_scales[:],
+                rhs=k_words[:].bitcast(FP4X4),
+                rhs_scale=k_bytes[:],
+                start=True,
+                stop=True,
+            )
+            nc.scalar.activation(sq[:, r, :], score[:], ACT.Square, accum_out=sums[:, r : r + 1])
+            nc.vector.tensor_scalar(
+                x[:, r, :], sq[:, r, :], floor_sb[:, r : r + 1], qs_sb[:, r : r + 1], ALU.add, ALU.mult
+            )
+        z = sb.tile([P, PACK], F32, name="z")
+        rz = sb.tile([P, PACK], F32, name="rz")
+        nc.vector.tensor_tensor(z[:], sums[:], base[:], ALU.add)
+        nc.vector.reciprocal(rz[:], z[:])
+        w_bf = sb.tile([P, I, PACK], BF16, name="w_bf", align_bytes=64)
+        nc.vector.tensor_tensor(
+            w_bf[:].rearrange("p (c i) r -> p c r i", i=4),
+            x[:].rearrange("p r (c i) -> p c r i", i=4),
+            rz[:].unsqueeze(1).unsqueeze(3).to_broadcast([P, I // 4, PACK, 4]),
+            ALU.mult,
+        )
+        w_codes = sb.tile([P, I], U32, name="w_codes", align_bytes=64)
+        w_scales = sb.tile([P, I], U8, name="w_scales", align_bytes=64)
+        nc.vector.quantize_mx(
+            out=w_codes[:].bitcast(FP8X4), scales=w_scales[:], in_=w_bf[:].rearrange("p i r -> p (i r)")
+        )
+
+        g_bf = sb.tile([P, E, PACK], BF16, name="g_bf", align_bytes=64)
+        nc.scalar.copy(
+            g_bf[:].rearrange("p (c i) j -> p c j i", i=4), g_raw[:].rearrange("p j (c i) -> p c j i", i=4)
+        )
+        g_codes = sb.tile([P, E], U32, name="g_codes", align_bytes=64)
+        g_scales = sb.tile([P, E], U8, name="g_scales", align_bytes=64)
+        nc.vector.quantize_mx(
+            out=g_codes[:].bitcast(FP8X4), scales=g_scales[:], in_=g_bf[:].rearrange("p e j -> p (e j)")
+        )
+
+        fade_ps = []
+        for h in range(2):
+            t = ps.tile([P, PACK, P], F32, name=f"fade_ps{h}")
+            for j in range(PACK):
+                nc.tensor.transpose(t[:, j, :], fade_cols[:, h, j : j + 1].to_broadcast([P, P]), ident[:])
+            fade_ps.append(t)
+
+        for c in range(E // P):
+            gv_ps = ps.tile([P, I], F32, name=f"gv_ps{c}", tag=f"bank{c}")
+            nc.tensor.matmul_mx(
+                out=gv_ps[:],
+                lhsT=g_codes[:, c * P : (c + 1) * P].bitcast(FP8X4),
+                lhsT_scale=g_scales[:, c * P : (c + 1) * P],
+                rhs=w_codes[:].bitcast(FP8X4),
+                rhs_scale=w_scales[:],
+                start=True,
+                stop=True,
+            )
+            gv = sb.tile([P, I], F32, name=f"gv{c}")
+            nc.scalar.copy(gv[:], gv_ps[:])
+            nc.vector.tensor_copy(windows[c][:].indirect(offsets[:]), gv[:])
+            for h in range(2):
+                part = acc[c][:, h * BANK : (h + 1) * BANK].rearrange("p (n j) -> p n j", j=PACK)
+                nc.vector.tensor_tensor(part, part, fade_ps[h][:].rearrange("p j n -> p n j"), ALU.mult)
+            if c < 3:
+                nc.gpsimd.tensor_tensor(acc[c][:], acc[c][:], windows[c][:], ALU.add)
+                nc.sync.dma_start(out[c * P : (c + 1) * P, :], acc[c][:])
+            else:
+                for h in range(2):
+                    cols = slice(h * BANK, (h + 1) * BANK)
+                    nc.vector.tensor_tensor(acc[c][:, cols], acc[c][:, cols], windows[c][:, cols], ALU.add)
+                    nc.sync.dma_start(out[c * P : (c + 1) * P, cols], acc[c][:, cols])

@@ -26,16 +26,20 @@ def tile_attend_bsquareshares_v_kernel(tc, query, keys_words, keys_scales, floor
     nc = tc.nc
     with ExitStack() as ctx:
         sb = ctx.enter_context(tc.tile_pool(name="sb", bufs=1))
+        hold = ctx.enter_context(tc.tile_pool(name="hold", bufs=1))
         ps = ctx.enter_context(tc.psum_pool(name="ps", bufs=1))
 
+        key_bytes = sb.tile([P, T], U8, name="key_bytes", align_bytes=64)
+        nc.gpsimd.memset(key_bytes[:].bitcast(I32), 0)
+        fade_rows = sb.tile([P, P], F32, name="fade_rows")
+        nc.gpsimd.memset(fade_rows[:], 0.0)
+        nc.sync.dma_start(fade_rows[0 : T // P, :], fade.rearrange("o (b n) -> (o b) n", n=P))
         offsets = sb.tile([P, I // 16], U16, name="offsets")
         nc.sync.dma_start(offsets[:], offs)
         key_words = sb.tile([P, T], U16, name="key_words", align_bytes=64)
         nc.sync.dma_start(key_words[:].bitcast(I32), keys_words[0].bitcast(I32))
-        key_bytes = sb.tile([P, T], U8, name="key_bytes", align_bytes=64)
-        nc.vector.memset(key_bytes[:].bitcast(I32), 0)
         for quad in range(4):
-            nc.scalar.dma_start(
+            nc.sync.dma_start(
                 key_bytes[32 * quad : 32 * quad + 4, :].bitcast(I32),
                 keys_scales[0, 4 * quad : 4 * quad + 4, :].bitcast(I32),
             )
@@ -48,10 +52,10 @@ def tile_attend_bsquareshares_v_kernel(tc, query, keys_words, keys_scales, floor
         floor_sb = sb.tile([P, PACK], F32, name="floor_sb")
         reserve_sb = sb.tile([P, PACK], F32, name="reserve_sb")
         qs_sb = sb.tile([P, PACK], F32, name="qs_sb")
+        ident = sb.tile([P, P], F32, name="ident")
+        make_identity(nc, ident[:])
         for t, src in ((floor_sb, floor), (reserve_sb, reserve), (qs_sb, qs)):
             nc.sync.dma_start(t[:], src.rearrange("(p r) o -> p (r o)", r=PACK))
-        fade_cols = sb.tile([P, 2, PACK], F32, name="fade_cols")
-        nc.sync.dma_start(fade_cols[:], fade.rearrange("o (h p j) -> p (o h) j", h=2, j=PACK))
         g_raw = sb.tile([P, PACK, E], F32, name="g_raw")
         nc.sync.dma_start(g_raw[:], grows.rearrange("(p j) e -> p j e", j=PACK))
         acc = []
@@ -61,12 +65,11 @@ def tile_attend_bsquareshares_v_kernel(tc, query, keys_words, keys_scales, floor
             acc.append(t)
 
         windows = []
-        for c in range(E // P):
+        for c in range(3):
             t = sb.tile([P, T], F32, name=f"window{c}")
-            nc.vector.memset(t[:], 0.0)
+            (nc.vector if c < 2 else nc.gpsimd).memset(t[:], 0.0)
             windows.append(t)
-        ident = sb.tile([P, P], F32, name="ident")
-        make_identity(nc, ident[:])
+        windows.append(windows[0])
 
         k_words = sb.tile([P, I], U16, name="k_words", align_bytes=64)
         k_bytes = sb.tile([P, I], U8, name="k_bytes", align_bytes=64)
@@ -81,6 +84,18 @@ def tile_attend_bsquareshares_v_kernel(tc, query, keys_words, keys_scales, floor
                 nc.scalar.copy(dst, src)
             else:
                 nc.vector.tensor_copy(dst, src)
+        halves = [slice(h * BANK, (h + 1) * BANK) for h in range(2)]
+        cols_ps = ps.tile([P, P], F32, name="cols_ps", tag="spare0")
+        nc.tensor.transpose(cols_ps[:], fade_rows[:], ident[:])
+        fade_cols = sb.tile([P, T // P], F32, name="fade_cols")
+        nc.scalar.copy(fade_cols[:], cols_ps[:, 0 : T // P])
+        fade_sb = sb.tile([P, T], F32, name="fade_sb")
+        for h in range(2):
+            t = ps.tile([P, PACK, P], F32, name=f"fade_ps{h}", tag=f"spare{1 + h}")
+            for j in range(PACK):
+                b = PACK * h + j
+                nc.tensor.transpose(t[:, j, :], fade_cols[:, b : b + 1].to_broadcast([P, P]), ident[:])
+            nc.scalar.copy(fade_sb[:, halves[h]], t[:].rearrange("p j n -> p (j n)"))
         base = sb.tile([P, PACK], F32, name="base")
         nc.vector.scalar_tensor_tensor(base[:], floor_sb[:], float(I), reserve_sb[:], ALU.mult, ALU.add)
 
@@ -111,7 +126,7 @@ def tile_attend_bsquareshares_v_kernel(tc, query, keys_words, keys_scales, floor
         rz = sb.tile([P, PACK], F32, name="rz")
         nc.vector.tensor_tensor(z[:], sums[:], base[:], ALU.add)
         nc.vector.reciprocal(rz[:], z[:])
-        w_bf = sb.tile([P, I, PACK], BF16, name="w_bf", align_bytes=64)
+        w_bf = hold.tile([P, I, PACK], BF16, name="w_bf", offset=0, align_bytes=64)
         nc.vector.tensor_tensor(
             w_bf[:].rearrange("p (c i) r -> p c r i", i=4),
             x[:].rearrange("p r (c i) -> p c r i", i=4),
@@ -124,29 +139,26 @@ def tile_attend_bsquareshares_v_kernel(tc, query, keys_words, keys_scales, floor
             out=w_codes[:].bitcast(FP8X4), scales=w_scales[:], in_=w_bf[:].rearrange("p i r -> p (i r)")
         )
 
-        g_bf = sb.tile([P, E, PACK], BF16, name="g_bf", align_bytes=64)
-        nc.scalar.copy(
-            g_bf[:].rearrange("p (c i) j -> p c j i", i=4), g_raw[:].rearrange("p j (c i) -> p c j i", i=4)
-        )
-        g_codes = sb.tile([P, E], U32, name="g_codes", align_bytes=64)
-        g_scales = sb.tile([P, E], U8, name="g_scales", align_bytes=64)
-        nc.vector.quantize_mx(
-            out=g_codes[:].bitcast(FP8X4), scales=g_scales[:], in_=g_bf[:].rearrange("p e j -> p (e j)")
-        )
-
-        fade_ps = []
-        for h in range(2):
-            t = ps.tile([P, PACK, P], F32, name=f"fade_ps{h}")
-            for j in range(PACK):
-                nc.tensor.transpose(t[:, j, :], fade_cols[:, h, j : j + 1].to_broadcast([P, P]), ident[:])
-            fade_ps.append(t)
-
+        gvs = []
         for c in range(E // P):
+            if c < 2:
+                g_bf = sb.tile([P, P, PACK], BF16, name=f"g_bf{c}", align_bytes=64)
+            else:
+                g_bf = hold.tile([P, P, PACK], BF16, name=f"g_bf{c}", offset=1024 * c, align_bytes=64)
+            nc.scalar.copy(
+                g_bf[:].rearrange("p (c i) j -> p c j i", i=4),
+                g_raw[:, :, c * P : (c + 1) * P].rearrange("p j (c i) -> p c j i", i=4),
+            )
+            g_codes = sb.tile([P, P], U32, name=f"g_codes{c}", align_bytes=64)
+            g_scales = sb.tile([P, P], U8, name=f"g_scales{c}", align_bytes=64)
+            nc.vector.quantize_mx(
+                out=g_codes[:].bitcast(FP8X4), scales=g_scales[:], in_=g_bf[:].rearrange("p e j -> p (e j)")
+            )
             gv_ps = ps.tile([P, I], F32, name=f"gv_ps{c}", tag=f"bank{c}")
             nc.tensor.matmul_mx(
                 out=gv_ps[:],
-                lhsT=g_codes[:, c * P : (c + 1) * P].bitcast(FP8X4),
-                lhsT_scale=g_scales[:, c * P : (c + 1) * P],
+                lhsT=g_codes[:].bitcast(FP8X4),
+                lhsT_scale=g_scales[:],
                 rhs=w_codes[:].bitcast(FP8X4),
                 rhs_scale=w_scales[:],
                 start=True,
@@ -154,15 +166,54 @@ def tile_attend_bsquareshares_v_kernel(tc, query, keys_words, keys_scales, floor
             )
             gv = sb.tile([P, I], F32, name=f"gv{c}")
             nc.scalar.copy(gv[:], gv_ps[:])
-            nc.vector.tensor_copy(windows[c][:].indirect(offsets[:]), gv[:])
+            gvs.append(gv)
+
+        turned = []
+        for k in range(4):
+            fwd = ps.tile([P, 2, 2, P], F32, name=f"fwd{k}", tag=f"bank{k}")
+            for u in range(2):
+                b = 2 * k + u
+                for v in range(2):
+                    nc.tensor.transpose(fwd[:, u, v, :], acc[2 + v][:, b * P : (b + 1) * P], ident[:])
+            for u in range(2):
+                b = 2 * k + u
+                t = sb.tile([P, 2, P], F32, name=f"turned{b}")
+                nc.scalar.activation(t[:], fwd[:, u], ACT.Copy, scale=fade_cols[:, b : b + 1])
+                turned.append(t)
+        back = {}
+        for v in range(2):
             for h in range(2):
-                part = acc[c][:, h * BANK : (h + 1) * BANK].rearrange("p (n j) -> p n j", j=PACK)
-                nc.vector.tensor_tensor(part, part, fade_ps[h][:].rearrange("p j n -> p n j"), ALU.mult)
-            if c < 3:
-                nc.gpsimd.tensor_tensor(acc[c][:], acc[c][:], windows[c][:], ALU.add)
-                nc.sync.dma_start(out[c * P : (c + 1) * P, :], acc[c][:])
-            else:
-                for h in range(2):
-                    cols = slice(h * BANK, (h + 1) * BANK)
-                    nc.vector.tensor_tensor(acc[c][:, cols], acc[c][:, cols], windows[c][:, cols], ALU.add)
-                    nc.sync.dma_start(out[c * P : (c + 1) * P, cols], acc[c][:, cols])
+                t = ps.tile([P, PACK, P], F32, name=f"back{v}{h}", tag=f"spare{2 * v + h}")
+                for j in range(PACK):
+                    nc.tensor.transpose(t[:, j, :], turned[PACK * h + j][:, v, :], ident[:])
+                back[2 + v, h] = t
+
+        def scatter(c):
+            nc.vector.tensor_copy(windows[c][:].indirect(offsets[:]), gvs[c][:])
+
+        def store(c, cols):
+            queue = nc.sync if c < 2 else nc.scalar
+            queue.dma_start(out[c * P : (c + 1) * P, cols], acc[c][:, cols])
+
+        def add_on_vector(c):
+            for h in range(2):
+                nc.vector.tensor_tensor(
+                    acc[c][:, halves[h]], back[c, h][:].rearrange("p j n -> p (j n)"), windows[c][:, halves[h]], ALU.add
+                )
+                store(c, halves[h])
+
+        faded0 = hold.tile([P, T], F32, name="faded0", offset=0, align_bytes=64)
+        nc.gpsimd.tensor_tensor(faded0[:], acc[0][:], fade_sb[:], ALU.mult)
+        scatter(0)
+        nc.gpsimd.tensor_tensor(acc[0][:], faded0[:], windows[0][:], ALU.add)
+        store(0, slice(0, T))
+        scatter(1)
+        faded1 = hold.tile([P, T], F32, name="faded1", offset=0, align_bytes=64)
+        for cols in halves:
+            nc.gpsimd.tensor_tensor(faded1[:, cols], acc[1][:, cols], fade_sb[:, cols], ALU.mult)
+            nc.gpsimd.tensor_tensor(acc[1][:, cols], faded1[:, cols], windows[1][:, cols], ALU.add)
+            store(1, cols)
+        scatter(2)
+        add_on_vector(2)
+        scatter(3)
+        add_on_vector(3)

from contextlib import ExitStack

import concourse.mybir as mybir
from concourse.masks import make_identity

D, E, T, I, Q = 512, 512, 1024, 256, 512
FLOPS = 2 * D * Q * I + 2 * Q * E * I

F32 = mybir.dt.float32
BF16 = mybir.dt.bfloat16
I32 = mybir.dt.int32
U32 = mybir.dt.uint32
U16 = mybir.dt.uint16
U8 = mybir.dt.uint8
FP8X4 = mybir.dt.float8_e4m3fn_x4
FP4X4 = mybir.dt.float4_e2m1fn_x4
ALU = mybir.AluOpType
ACT = mybir.ActivationFunctionType

P = 128
PACK = 4
BANK = 512


def tile_attend_bsquareshares_v_kernel(tc, query, keys_words, keys_scales, floor, reserve, qs, grows, old, fade, offs, out):
    nc = tc.nc
    with ExitStack() as ctx:
        sb = ctx.enter_context(tc.tile_pool(name="sb", bufs=1))
        hold = ctx.enter_context(tc.tile_pool(name="hold", bufs=1))
        ps = ctx.enter_context(tc.psum_pool(name="ps", bufs=1))

        key_bytes = sb.tile([P, T], U8, name="key_bytes", align_bytes=64)
        nc.gpsimd.memset(key_bytes[:].bitcast(I32), 0)
        fade_rows = sb.tile([P, P], F32, name="fade_rows")
        nc.gpsimd.memset(fade_rows[:], 0.0)
        nc.sync.dma_start(fade_rows[0 : T // P, :], fade.rearrange("o (b n) -> (o b) n", n=P))
        offsets = sb.tile([P, I // 16], U16, name="offsets")
        nc.sync.dma_start(offsets[:], offs)
        key_words = sb.tile([P, T], U16, name="key_words", align_bytes=64)
        nc.sync.dma_start(key_words[:].bitcast(I32), keys_words[0].bitcast(I32))
        for quad in range(4):
            nc.sync.dma_start(
                key_bytes[32 * quad : 32 * quad + 4, :].bitcast(I32),
                keys_scales[0, 4 * quad : 4 * quad + 4, :].bitcast(I32),
            )
        q_rows = query.rearrange("(p j) q -> p j q", j=PACK)
        q_raw = []
        for h in range(2):
            t = sb.tile([P, PACK, Q // 2], F32, name=f"q_raw{h}")
            nc.sync.dma_start(t[:], q_rows[:, :, h * (Q // 2) : (h + 1) * (Q // 2)])
            q_raw.append(t)
        floor_sb = sb.tile([P, PACK], F32, name="floor_sb")
        reserve_sb = sb.tile([P, PACK], F32, name="reserve_sb")
        qs_sb = sb.tile([P, PACK], F32, name="qs_sb")
        ident = sb.tile([P, P], F32, name="ident")
        make_identity(nc, ident[:])
        for t, src in ((floor_sb, floor), (reserve_sb, reserve), (qs_sb, qs)):
            nc.sync.dma_start(t[:], src.rearrange("(p r) o -> p (r o)", r=PACK))
        g_raw = sb.tile([P, PACK, E], F32, name="g_raw")
        nc.sync.dma_start(g_raw[:], grows.rearrange("(p j) e -> p j e", j=PACK))
        acc = []
        for c in range(E // P):
            t = sb.tile([P, T], F32, name=f"acc{c}")
            nc.sync.dma_start(t[:], old[c * P : (c + 1) * P, :])
            acc.append(t)

        windows = []
        for c in range(3):
            t = sb.tile([P, T], F32, name=f"window{c}")
            (nc.vector if c < 2 else nc.gpsimd).memset(t[:], 0.0)
            windows.append(t)
        windows.append(windows[0])

        k_words = sb.tile([P, I], U16, name="k_words", align_bytes=64)
        k_bytes = sb.tile([P, I], U8, name="k_bytes", align_bytes=64)
        nc.vector.tensor_copy(k_words[:], key_words[:].indirect(offsets[:]))
        nc.vector.tensor_copy(k_bytes[:], key_bytes[:].indirect(offsets[:]))

        q_bf = sb.tile([P, PACK, P, PACK], BF16, name="q_bf", align_bytes=64)
        for h in range(2):
            dst = q_bf[:, :, h * 64 : (h + 1) * 64, :].rearrange("p r s j -> p s j r")
            src = q_raw[h][:].rearrange("p j (s r) -> p s j r", r=PACK)
            if h == 0:
                nc.scalar.copy(dst, src)
            else:
                nc.vector.tensor_copy(dst, src)
        halves = [slice(h * BANK, (h + 1) * BANK) for h in range(2)]
        cols_ps = ps.tile([P, P], F32, name="cols_ps", tag="spare0")
        nc.tensor.transpose(cols_ps[:], fade_rows[:], ident[:])
        fade_cols = sb.tile([P, T // P], F32, name="fade_cols")
        nc.scalar.copy(fade_cols[:], cols_ps[:, 0 : T // P])
        fade_sb = sb.tile([P, T], F32, name="fade_sb")
        for h in range(2):
            t = ps.tile([P, PACK, P], F32, name=f"fade_ps{h}", tag=f"spare{1 + h}")
            for j in range(PACK):
                b = PACK * h + j
                nc.tensor.transpose(t[:, j, :], fade_cols[:, b : b + 1].to_broadcast([P, P]), ident[:])
            nc.scalar.copy(fade_sb[:, halves[h]], t[:].rearrange("p j n -> p (j n)"))
        base = sb.tile([P, PACK], F32, name="base")
        nc.vector.scalar_tensor_tensor(base[:], floor_sb[:], float(I), reserve_sb[:], ALU.mult, ALU.add)

        sq = sb.tile([P, PACK, I], F32, name="sq")
        x = sb.tile([P, PACK, I], F32, name="x")
        sums = sb.tile([P, PACK], F32, name="sums")
        for r in range(PACK):
            q_codes = sb.tile([P, P], U32, name=f"q_codes{r}", align_bytes=64)
            q_scales = sb.tile([P, P], U8, name=f"q_scales{r}", align_bytes=64)
            nc.vector.quantize_mx(
                out=q_codes[:].bitcast(FP8X4), scales=q_scales[:], in_=q_bf[:, r].rearrange("p s j -> p (s j)")
            )
            score = ps.tile([P, I], F32, name=f"score{r}", tag=f"bank{r}")
            nc.tensor.matmul_mx(
                out=score[:],
                lhsT=q_codes[:].bitcast(FP8X4),
                lhsT_scale=q_scales[:],
                rhs=k_words[:].bitcast(FP4X4),
                rhs_scale=k_bytes[:],
                start=True,
                stop=True,
            )
            nc.scalar.activation(sq[:, r, :], score[:], ACT.Square, accum_out=sums[:, r : r + 1])
            nc.vector.tensor_scalar(
                x[:, r, :], sq[:, r, :], floor_sb[:, r : r + 1], qs_sb[:, r : r + 1], ALU.add, ALU.mult
            )
        z = sb.tile([P, PACK], F32, name="z")
        rz = sb.tile([P, PACK], F32, name="rz")
        nc.vector.tensor_tensor(z[:], sums[:], base[:], ALU.add)
        nc.vector.reciprocal(rz[:], z[:])
        w_bf = hold.tile([P, I, PACK], BF16, name="w_bf", offset=0, align_bytes=64)
        nc.vector.tensor_tensor(
            w_bf[:].rearrange("p (c i) r -> p c r i", i=4),
            x[:].rearrange("p r (c i) -> p c r i", i=4),
            rz[:].unsqueeze(1).unsqueeze(3).to_broadcast([P, I // 4, PACK, 4]),
            ALU.mult,
        )
        w_codes = sb.tile([P, I], U32, name="w_codes", align_bytes=64)
        w_scales = sb.tile([P, I], U8, name="w_scales", align_bytes=64)
        nc.vector.quantize_mx(
            out=w_codes[:].bitcast(FP8X4), scales=w_scales[:], in_=w_bf[:].rearrange("p i r -> p (i r)")
        )

        gvs = []
        for c in range(E // P):
            if c < 2:
                g_bf = sb.tile([P, P, PACK], BF16, name=f"g_bf{c}", align_bytes=64)
            else:
                g_bf = hold.tile([P, P, PACK], BF16, name=f"g_bf{c}", offset=1024 * c, align_bytes=64)
            nc.scalar.copy(
                g_bf[:].rearrange("p (c i) j -> p c j i", i=4),
                g_raw[:, :, c * P : (c + 1) * P].rearrange("p j (c i) -> p c j i", i=4),
            )
            g_codes = sb.tile([P, P], U32, name=f"g_codes{c}", align_bytes=64)
            g_scales = sb.tile([P, P], U8, name=f"g_scales{c}", align_bytes=64)
            nc.vector.quantize_mx(
                out=g_codes[:].bitcast(FP8X4), scales=g_scales[:], in_=g_bf[:].rearrange("p e j -> p (e j)")
            )
            gv_ps = ps.tile([P, I], F32, name=f"gv_ps{c}", tag=f"bank{c}")
            nc.tensor.matmul_mx(
                out=gv_ps[:],
                lhsT=g_codes[:].bitcast(FP8X4),
                lhsT_scale=g_scales[:],
                rhs=w_codes[:].bitcast(FP8X4),
                rhs_scale=w_scales[:],
                start=True,
                stop=True,
            )
            gv = sb.tile([P, I], F32, name=f"gv{c}")
            nc.scalar.copy(gv[:], gv_ps[:])
            gvs.append(gv)

        turned = []
        for k in range(4):
            fwd = ps.tile([P, 2, 2, P], F32, name=f"fwd{k}", tag=f"bank{k}")
            for u in range(2):
                b = 2 * k + u
                for v in range(2):
                    nc.tensor.transpose(fwd[:, u, v, :], acc[2 + v][:, b * P : (b + 1) * P], ident[:])
            for u in range(2):
                b = 2 * k + u
                t = sb.tile([P, 2, P], F32, name=f"turned{b}")
                nc.scalar.activation(t[:], fwd[:, u], ACT.Copy, scale=fade_cols[:, b : b + 1])
                turned.append(t)
        back = {}
        for v in range(2):
            for h in range(2):
                t = ps.tile([P, PACK, P], F32, name=f"back{v}{h}", tag=f"spare{2 * v + h}")
                for j in range(PACK):
                    nc.tensor.transpose(t[:, j, :], turned[PACK * h + j][:, v, :], ident[:])
                back[2 + v, h] = t

        def scatter(c):
            nc.vector.tensor_copy(windows[c][:].indirect(offsets[:]), gvs[c][:])

        def store(c, cols):
            queue = nc.sync if c < 2 else nc.scalar
            queue.dma_start(out[c * P : (c + 1) * P, cols], acc[c][:, cols])

        def add_on_vector(c):
            for h in range(2):
                nc.vector.tensor_tensor(
                    acc[c][:, halves[h]], back[c, h][:].rearrange("p j n -> p (j n)"), windows[c][:, halves[h]], ALU.add
                )
                store(c, halves[h])

        faded0 = hold.tile([P, T], F32, name="faded0", offset=0, align_bytes=64)
        nc.gpsimd.tensor_tensor(faded0[:], acc[0][:], fade_sb[:], ALU.mult)
        scatter(0)
        nc.gpsimd.tensor_tensor(acc[0][:], faded0[:], windows[0][:], ALU.add)
        store(0, slice(0, T))
        scatter(1)
        faded1 = hold.tile([P, T], F32, name="faded1", offset=0, align_bytes=64)
        for cols in halves:
            nc.gpsimd.tensor_tensor(faded1[:, cols], acc[1][:, cols], fade_sb[:, cols], ALU.mult)
            nc.gpsimd.tensor_tensor(acc[1][:, cols], faded1[:, cols], windows[1][:, cols], ALU.add)
            store(1, cols)
        scatter(2)
        add_on_vector(2)
        scatter(3)
        add_on_vector(3)
